import numpy as np
import ml_dtypes


def mxq(x, axis, fmt="e4m3"):
    dtype, down = {"e4m3": (ml_dtypes.float8_e4m3fn, 7), "e5m2": (ml_dtypes.float8_e5m2, 14)}[fmt]
    v = np.moveaxis(np.asarray(x, np.float32).astype(ml_dtypes.bfloat16).astype(np.float64), axis, -1)
    blocks = v.reshape(v.shape[:-1] + (-1, 32))
    amax = np.abs(blocks).max(-1, keepdims=True)
    byte = np.maximum(np.where(amax > 0, np.frexp(amax)[1] - 1 + 127, 0) - down, 1)
    scale = np.exp2(byte - 127.0)
    codes = (blocks / scale).astype(np.float32).astype(dtype).astype(np.float64)
    return np.moveaxis((codes * scale).reshape(v.shape), -1, axis)


WIDE = False


def mx_kscale(k):
    if not WIDE:
        return np.ones(k)
    levels = np.array([24, -24, 12, -12, 0])
    if k % 512:
        return np.exp2(np.random.permutation(np.resize(levels, k // 32))).repeat(32)
    a = np.empty((k // 512, 16))
    for p in range(k // 512):
        a[p, :8] = np.random.permutation(np.resize(levels, 8))
        for g in range(8):
            far = levels[np.abs(levels - a[p, g]) >= 10]
            a[p, g + 8] = far[np.random.randint(len(far))]
    return np.exp2(a.ravel()).repeat(32)


def f64(x):
    return np.asarray(x).astype(np.float64)


def striped(idx):
    return np.tile(idx.reshape(-1, 16).T, (8, 1)).astype(np.uint16)


def unstriped(offs):
    return offs[:16].T.reshape(-1).astype(np.int64)


E2M1 = np.array([0.0, 0.5, 1.0, 1.5, 2.0, 3.0, 4.0, 6.0, -0.0, -0.5, -1.0, -1.5, -2.0, -3.0, -4.0, -6.0])


def pack_weight(w, fmt):
    k, n = w.shape
    w = f64(np.asarray(w, np.float32).astype(ml_dtypes.bfloat16)).reshape(k // 32, 32, n)
    amax = np.abs(w).max(1)
    if fmt == "e4m3":
        byte = np.frexp(amax)[1] - 1 + 127 - 7
    else:
        mant, ex = np.frexp(amax / 6.0)
        byte = np.where(mant > 0.5, ex, ex - 1) + 127
    byte = np.clip(np.where(amax > 0, byte, 1), 1, 254)
    scaled = (w * np.exp2(127.0 - byte)[:, None, :]).reshape(k, n).astype(np.float32)
    by_word = np.ascontiguousarray(scaled.reshape(k // 512, 128, 4, n).transpose(0, 1, 3, 2))
    if fmt == "e4m3":
        words = by_word.astype(ml_dtypes.float8_e4m3fn).view(np.uint8)
    else:
        c = by_word.astype(ml_dtypes.float4_e2m1fn).view(np.uint8) & 0xF
        words = (c[..., 0::2] | (c[..., 1::2] << 4)).reshape(k // 512, 128, 2 * n)
    return np.ascontiguousarray(words), np.ascontiguousarray(byte.astype(np.uint8).reshape(k // 512, 16, n))


def unpack_weight(words, scales, fmt):
    g, _, n = scales.shape
    words = np.ascontiguousarray(words).reshape(g, 128, n, -1)
    if fmt == "e4m3":
        vals = words.view(ml_dtypes.float8_e4m3fn).astype(np.float64)
    else:
        nib = np.empty((g, 128, n, 4), np.uint8)
        nib[..., 0::2] = words & 0xF
        nib[..., 1::2] = words >> 4
        vals = E2M1[nib]
    vals = vals * np.repeat(np.exp2(scales.astype(np.float64) - 127.0), 8, axis=1)[..., None]
    return vals.transpose(0, 1, 3, 2).reshape(g * 512, n)


def pack_table4(v):
    words, scales = pack_weight(v, "e2m1")
    g, t = words.shape[0] // 2, v.shape[1]
    return np.ascontiguousarray(words.reshape(g, 2, 128, t, 2).transpose(0, 2, 3, 1, 4).reshape(g, 128, t, 4)), scales


def unpack_table4(words, scales):
    g, _, t, _ = words.shape
    return unpack_weight(words.reshape(g, 128, t, 2, 2).transpose(0, 3, 1, 2, 4).reshape(2 * g, 128, 2 * t), scales, "e2m1")


K, R, N, T, J = 1024, 512, 256, 2048, 512


def setup_inputs():
    n = np.random.standard_normal
    s = mx_kscale(K)[:, None]
    u = mx_kscale(R)[:, None]
    p_tab = pack_table4(n((K, T)) * s)
    p_w = pack_weight(n((K, R)) / np.sqrt(K) / s * u.T, "e4m3")
    p_wd = pack_weight(n((R, N)) / np.sqrt(R) / u, "e2m1")
    return {
        "tab_words": p_tab[0],
        "tab_scales": p_tab[1],
        "c": (n((K, J)) * s).astype(np.float32),
        "w_words": p_w[0],
        "w_scales": p_w[1],
        "wc": (n((K, R)) / np.sqrt(K) / s * u.T).astype(np.float32),
        "wd_words": p_wd[0],
        "wd_scales": p_wd[1],
        "b": (0.3 * n(N)).astype(np.float32),
        "offs": striped(np.concatenate([np.random.permutation(T)[:J] for _ in range(2)])),
    }


def reference(tab_words, tab_scales, c, w_words, w_scales, wc, wd_words, wd_scales, b, offs):
    idx = unstriped(offs).reshape(2, J)
    tab_ = unpack_table4(tab_words, tab_scales)[:, idx]
    c_ = mxq(f64(c), 0, "e4m3")
    w_ = unpack_weight(w_words, w_scales, "e4m3")
    a0 = w_.T @ tab_[:, 0]
    a1 = w_.T @ tab_[:, 1]
    wc_ = mxq(f64(wc), 0, "e4m3")
    ac = wc_.T @ c_
    h = np.maximum(np.maximum(a0, a1) + ac, 0.0)
    h_ = mxq(h, 0, "e4m3")
    wd_ = unpack_weight(wd_words, wd_scales, "e2m1")
    y = wd_.T @ h_
    return y + f64(b)[:, None]

@@ -1,0 +1,217 @@
+from contextlib import ExitStack
+
+import concourse.mybir as mybir
+
+K, R, N, T, J = 1024, 512, 256, 2048, 512
+FLOPS = 2 * (3 * K * R * J + R * N * J)
+
+F32 = mybir.dt.float32
+BF16 = mybir.dt.bfloat16
+I32 = mybir.dt.int32
+U32 = mybir.dt.uint32
+U16 = mybir.dt.uint16
+U8 = mybir.dt.uint8
+FP8X4 = mybir.dt.float8_e4m3fn_x4
+FP4X4 = mybir.dt.float4_e2m1fn_x4
+ALU = mybir.AluOpType
+ACT = mybir.ActivationFunctionType
+
+P = 128
+PACK = 4
+KP = P * PACK
+PASSES = K // KP
+CH = 128
+SHIFT = 16
+
+
+def tile_list_pnet_bias_kernel(
+    tc, tab_words, tab_scales, c, w_words, w_scales, wc, wd_words, wd_scales, b, offs, out
+):
+    nc = tc.nc
+    with ExitStack() as ctx:
+        keep = ctx.enter_context(tc.tile_pool(name="keep", bufs=1))
+        ring = ctx.enter_context(tc.tile_pool(name="ring", bufs=2))
+        psum = ctx.enter_context(tc.psum_pool(name="psum", bufs=2))
+
+        offsets = keep.tile([P, 2 * J // 16], U16, name="offsets")
+        tab_s = keep.tile([P, T], U8, name="tab_s", tag="reused", align_bytes=64)
+        tab_w = keep.tile([P, T], I32, name="tab_w", align_bytes=64)
+        got_s = keep.tile([P, 2 * J], U8, name="got_s", align_bytes=64)
+        got_s1 = keep.tile([P, 2 * J], U8, name="got_s1", align_bytes=64)
+        w_raw = keep.tile([P, PASSES, R], I32, name="w_raw", align_bytes=64)
+        ws_raw = keep.tile([P, PASSES, R], U8, name="ws_raw", align_bytes=64)
+        w_q = keep.tile([P, PASSES, R], I32, name="w_q", align_bytes=64)
+        w_s = keep.tile([P, PASSES, R], U8, name="w_s", align_bytes=64)
+        wd_q = keep.tile([P, 2 * N], U8, name="wd_q", align_bytes=64)
+        wd_s = keep.tile([P, N], U8, name="wd_s", align_bytes=64)
+        warm_in = keep.tile([P, 8], F32, name="warm_in")
+        warm_out = keep.tile([P, 8], F32, name="warm_out")
+
+        nc.vector.memset(tab_s[:].bitcast(I32), 0)
+        nc.vector.memset(ws_raw[:].rearrange("p a r -> p (a r)").bitcast(I32), 0)
+        nc.vector.memset(got_s1[:].bitcast(I32), 0)
+        nc.gpsimd.memset(warm_in[:], 0.0)
+        nc.gpsimd.memset(wd_s[:].bitcast(I32), 0)
+        nc.scalar.activation(out=warm_out[:], in_=warm_in[:], func=ACT.Identity, bias=warm_in[:, 0:1])
+
+        nc.sync.dma_start(offsets[:], offs)
+        ts32 = tab_scales.bitcast(I32).rearrange("a (q r) t -> r q a t", r=4)
+        for r in range(4):
+            nc.sync.dma_start(out=tab_s[r:P:SHIFT, :].bitcast(I32), in_=ts32[r])
+        nc.sync.dma_start(out=tab_w[:], in_=tab_words[0].rearrange("p t b -> p (t b)").bitcast(I32))
+
+        def load_rows(raw, src, a, lo, hi):
+            nc.sync.dma_start(out=raw, in_=src[a * KP : (a + 1) * KP, lo:hi].rearrange("(p i) w -> p i w", i=PACK))
+            return raw
+
+        half = R // 2
+        wc_raw = {}
+        early = keep.tile([P, 2, PACK, half], F32, name="early")
+        for h in range(2):
+            wc_raw[0, h] = load_rows(early[:, h], wc, 0, h * half, (h + 1) * half)
+        nc.sync.dma_start(out=w_raw[:], in_=w_words.rearrange("a p r i -> p a (r i)").bitcast(I32))
+        ws32 = w_scales.bitcast(I32).rearrange("a q r -> q a r")
+        for q in range(4):
+            nc.sync.dma_start(out=ws_raw[32 * q : 32 * q + 4].bitcast(I32), in_=ws32[4 * q : 4 * q + 4])
+        for q in range(4):
+            nc.gpsimd.dma_start(out=wd_s[32 * q : 32 * q + 4, :].bitcast(I32), in_=wd_scales[0, 4 * q : 4 * q + 4, :].bitcast(I32))
+        nc.gpsimd.dma_start(out=wd_q[:].bitcast(I32), in_=wd_words[0].bitcast(I32))
+
+        nc.vector.tensor_copy(out=got_s[:], in_=tab_s[:].indirect(offsets[:]))
+        nc.scalar.dma_start(out=got_s1[0 : P - SHIFT, :].bitcast(I32), in_=got_s[SHIFT:P, :].bitcast(I32))
+
+        late = keep.tile([P, PACK * R + PASSES * PACK * J + 16], F32, name="late", tag="reused", align_bytes=64)
+        for h in range(2):
+            wc_raw[1, h] = load_rows(late[:, h * PACK * half : (h + 1) * PACK * half].rearrange("p (i w) -> p i w", i=PACK), wc, 1, h * half, (h + 1) * half)
+        bias = late[:, PACK * R + PASSES * PACK * J :]
+        with nc.allow_non_contiguous_dma(reason="one bias value to a partition"):
+            nc.sync.dma_start(out=bias[:, 0 : N // P], in_=b.rearrange("(h p) -> p h", p=P))
+        pieces = [(0, 0, 256), (1, 0, 256), (0, 256, 512), (1, 256, 384), (1, 384, 512)]
+        c_raw = []
+        for a, lo, hi in pieces:
+            at = PACK * (R + a * J)
+            c_raw.append(load_rows(late[:, at + PACK * lo : at + PACK * hi].rearrange("p (i w) -> p i w", i=PACK), c, a, lo, hi))
+
+        cols = J // 16
+        v_q = []
+        got_w = []
+        for g in range(2):
+            gw = keep.tile([P, J], I32, name="got_w%d" % g, align_bytes=64)
+            nc.vector.tensor_copy(out=gw[:].bitcast(U32), in_=tab_w[:].bitcast(U32).indirect(offsets[:, g * cols : (g + 1) * cols]))
+            got_w.append(gw)
+        for g in range(2):
+            vq = keep.tile([P, PASSES, 2 * J], U8, name="v_q%d" % g, align_bytes=64)
+            nc.vector.tensor_copy(out=vq[:].bitcast(U16), in_=got_w[g][:].bitcast(U16).rearrange("p (j d) -> p d j", d=2))
+            v_q.append(vq)
+
+        for a in range(PASSES):
+            nc.vector.tensor_copy(
+                out=w_q[:, a, :].rearrange("p (t c i) -> p c t i", t=4, i=4),
+                in_=w_raw[:, a, :].rearrange("p (c i t) -> p c t i", t=4, i=4),
+            )
+        nc.vector.tensor_copy(
+            out=w_s[:].rearrange("p a (t m) -> p a t m", t=4),
+            in_=ws_raw[:].rearrange("p a (m t) -> p a t m", t=4),
+        )
+
+        wc_q = keep.tile([P, PASSES, R], U32, name="wc_q", align_bytes=64)
+        wc_s = keep.tile([P, PASSES, R], U8, name="wc_s", align_bytes=64)
+        wc_g = [keep.tile([P, 4, P, PACK], BF16, name="wc_g%d" % a, align_bytes=64) for a in range(PASSES)]
+
+        def wc_pass(a):
+            for h in range(2):
+                nc.scalar.copy(
+                    out=wc_g[a][:, :, h * 64 : (h + 1) * 64, :].rearrange("p t m i -> p m i t"),
+                    in_=wc_raw[a, h].rearrange("p i (m t) -> p m i t", t=4),
+                )
+            nc.vector.quantize_mx(out=wc_q[:, a, :].bitcast(FP8X4), scales=wc_s[:, a, :], in_=wc_g[a][:].rearrange("p t m i -> p (t m i)"))
+
+        wc_pass(0)
+        wc_pass(1)
+
+        pooled = keep.tile([P, 4, J], F32, name="pooled")
+        planes = [got_s, got_s1]
+        for t in range(4):
+            banks = []
+            for g in range(2):
+                bank = psum.tile([P, J], F32, name="nb%d" % g)
+                for a in range(PASSES):
+                    nc.tensor.matmul_mx(
+                        out=bank[:],
+                        lhsT=w_q[:, a, t * P : (t + 1) * P].bitcast(FP8X4),
+                        lhsT_scale=w_s[:, a, t * P : (t + 1) * P],
+                        rhs=v_q[g][:, a, :].bitcast(FP4X4),
+                        rhs_scale=planes[a][:, g * J : (g + 1) * J],
+                        start=(a == 0),
+                        stop=(a == PASSES - 1),
+                    )
+                banks.append(bank)
+            first = ring.tile([P, J], F32, name="first")
+            nc.scalar.copy(out=first[:], in_=banks[0][:])
+            nc.vector.tensor_tensor(out=pooled[:, t, :], in0=banks[1][:], in1=first[:], op=ALU.max)
+
+        c_q = keep.tile([P, PASSES, J], U32, name="c_q", align_bytes=64)
+        c_s = keep.tile([P, PASSES, J], U8, name="c_s", align_bytes=64)
+        c_g = keep.tile([P, PASSES, J, PACK], BF16, name="c_g", align_bytes=64)
+
+        def c_piece(n):
+            a, lo, hi = pieces[n]
+            dst = c_g[:, a, lo:hi, :].rearrange("p (c j) i -> p c i j", j=4)
+            src = c_raw[n].rearrange("p i (c j) -> p c i j", j=4)
+            if n == len(pieces) - 1:
+                nc.vector.tensor_copy(out=dst, in_=src)
+            else:
+                nc.scalar.copy(out=dst, in_=src)
+            nc.vector.quantize_mx(out=c_q[:, a, lo:hi].bitcast(FP8X4), scales=c_s[:, a, lo:hi], in_=c_g[:, a, lo:hi, :].rearrange("p j i -> p (j i)"))
+
+        def chunk(n):
+            tok = slice(n * CH, (n + 1) * CH)
+            own = psum.tile([P, 4, CH], F32, name="own")
+            for t in range(4):
+                for a in range(PASSES):
+                    nc.tensor.matmul_mx(
+                        out=own[:, t, :],
+                        lhsT=wc_q[:, a, t * P : (t + 1) * P].bitcast(FP8X4),
+                        lhsT_scale=wc_s[:, a, t * P : (t + 1) * P],
+                        rhs=c_q[:, a, tok].bitcast(FP8X4),
+                        rhs_scale=c_s[:, a, tok],
+                        start=(a == 0),
+                        stop=(a == PASSES - 1),
+                    )
+            z = ring.tile([P, CH, PACK], BF16, name="z", align_bytes=64)
+            nc.vector.tensor_tensor(
+                out=z[:].rearrange("p (c j) t -> p c t j", j=4),
+                in0=own[:].rearrange("p t (c j) -> p c t j", j=4),
+                in1=pooled[:, :, tok].rearrange("p t (c j) -> p c t j", j=4),
+                op=ALU.add,
+            )
+            hid = ring.tile([P, CH * PACK], BF16, name="hid", align_bytes=64)
+            nc.vector.tensor_scalar_max(out=hid[:], in0=z[:].rearrange("p j t -> p (j t)"), scalar1=0.0)
+            h_q = ring.tile([P, CH], U32, name="h_q", align_bytes=64)
+            h_s = ring.tile([P, CH], U8, name="h_s", align_bytes=64)
+            nc.vector.quantize_mx(out=h_q[:].bitcast(FP8X4), scales=h_s[:], in_=hid[:])
+            y = psum.tile([P, N // P, CH], F32, name="y")
+            res = ring.tile([P, N // P, CH], F32, name="res")
+            for h in range(N // P):
+                nc.tensor.matmul_mx(
+                    out=y[:, h, :],
+                    lhsT=wd_q[:, 2 * h * P : 2 * (h + 1) * P].bitcast(FP4X4),
+                    lhsT_scale=wd_s[:, h * P : (h + 1) * P],
+                    rhs=h_q[:].bitcast(FP8X4),
+                    rhs_scale=h_s[:],
+                    start=True,
+                    stop=True,
+                )
+            for h in range(N // P):
+                nc.scalar.activation(out=res[:, h, :], in_=y[:, h, :], func=ACT.Identity, bias=bias[:, h : h + 1])
+            nc.sync.dma_start(out=out[:, tok].rearrange("(h p) j -> p h j", p=P), in_=res[:])
+
+        c_piece(0)
+        c_piece(1)
+        c_piece(2)
+        chunk(0)
+        c_piece(3)
+        chunk(1)
+        c_piece(4)
+        chunk(2)
+        chunk(3)

@@ -22,6 +22,7 @@ KP = P * PACK
 PASSES = K // KP
 CH = 128
 SHIFT = 16
+ON_VECTOR = (1,)
 
 
 def tile_list_pnet_bias_kernel(
@@ -30,11 +31,10 @@ def tile_list_pnet_bias_kernel(
     nc = tc.nc
     with ExitStack() as ctx:
         keep = ctx.enter_context(tc.tile_pool(name="keep", bufs=1))
-        ring = ctx.enter_context(tc.tile_pool(name="ring", bufs=2))
-        psum = ctx.enter_context(tc.psum_pool(name="psum", bufs=2))
+        psum = ctx.enter_context(tc.psum_pool(name="psum", bufs=8))
 
         offsets = keep.tile([P, 2 * J // 16], U16, name="offsets")
-        tab_s = keep.tile([P, T], U8, name="tab_s", tag="reused", align_bytes=64)
+        tab_s = keep.tile([P, T], U8, name="tab_s", align_bytes=64)
         tab_w = keep.tile([P, T], I32, name="tab_w", align_bytes=64)
         got_s = keep.tile([P, 2 * J], U8, name="got_s", align_bytes=64)
         got_s1 = keep.tile([P, 2 * J], U8, name="got_s1", align_bytes=64)
@@ -44,75 +44,72 @@ def tile_list_pnet_bias_kernel(
         w_s = keep.tile([P, PASSES, R], U8, name="w_s", align_bytes=64)
         wd_q = keep.tile([P, 2 * N], U8, name="wd_q", align_bytes=64)
         wd_s = keep.tile([P, N], U8, name="wd_s", align_bytes=64)
+        bias = keep.tile([P, N // P], F32, name="bias")
         warm_in = keep.tile([P, 8], F32, name="warm_in")
         warm_out = keep.tile([P, 8], F32, name="warm_out")
 
-        nc.vector.memset(tab_s[:].bitcast(I32), 0)
-        nc.vector.memset(ws_raw[:].rearrange("p a r -> p (a r)").bitcast(I32), 0)
-        nc.vector.memset(got_s1[:].bitcast(I32), 0)
+        nc.gpsimd.memset(tab_s[:].bitcast(I32), 0)
         nc.gpsimd.memset(warm_in[:], 0.0)
-        nc.gpsimd.memset(wd_s[:].bitcast(I32), 0)
-        nc.scalar.activation(out=warm_out[:], in_=warm_in[:], func=ACT.Identity, bias=warm_in[:, 0:1])
+        nc.vector.memset(ws_raw[:].rearrange("p a r -> p (a r)").bitcast(I32), 0)
+        nc.vector.memset(wd_s[:].bitcast(I32), 0)
+        nc.vector.memset(got_s1[:].bitcast(I32), 0)
 
         nc.sync.dma_start(offsets[:], offs)
+        nc.sync.dma_start(out=wd_q[:].bitcast(I32), in_=wd_words[0].bitcast(I32))
         ts32 = tab_scales.bitcast(I32).rearrange("a (q r) t -> r q a t", r=4)
         for r in range(4):
             nc.sync.dma_start(out=tab_s[r:P:SHIFT, :].bitcast(I32), in_=ts32[r])
+        nc.scalar.activation(out=warm_out[:], in_=warm_in[:], func=ACT.Identity, bias=warm_in[:, 0:1])
         nc.sync.dma_start(out=tab_w[:], in_=tab_words[0].rearrange("p t b -> p (t b)").bitcast(I32))
 
-        def load_rows(raw, src, a, lo, hi):
-            nc.sync.dma_start(out=raw, in_=src[a * KP : (a + 1) * KP, lo:hi].rearrange("(p i) w -> p i w", i=PACK))
+        def load_rows(src, a, lo, hi, name):
+            raw = keep.tile([P, PACK, hi - lo], F32, name=name, tag=name)
+            nc.sync.dma_start(out=raw[:], in_=src[a * KP : (a + 1) * KP, lo:hi].rearrange("(p i) w -> p i w", i=PACK))
             return raw
 
-        half = R // 2
-        wc_raw = {}
-        early = keep.tile([P, 2, PACK, half], F32, name="early")
-        for h in range(2):
-            wc_raw[0, h] = load_rows(early[:, h], wc, 0, h * half, (h + 1) * half)
-        nc.sync.dma_start(out=w_raw[:], in_=w_words.rearrange("a p r i -> p a (r i)").bitcast(I32))
         ws32 = w_scales.bitcast(I32).rearrange("a q r -> q a r")
         for q in range(4):
             nc.sync.dma_start(out=ws_raw[32 * q : 32 * q + 4].bitcast(I32), in_=ws32[4 * q : 4 * q + 4])
-        for q in range(4):
-            nc.gpsimd.dma_start(out=wd_s[32 * q : 32 * q + 4, :].bitcast(I32), in_=wd_scales[0, 4 * q : 4 * q + 4, :].bitcast(I32))
-        nc.gpsimd.dma_start(out=wd_q[:].bitcast(I32), in_=wd_words[0].bitcast(I32))
+        nc.sync.dma_start(out=w_raw[:], in_=w_words.rearrange("a p r i -> p a (r i)").bitcast(I32))
 
         nc.vector.tensor_copy(out=got_s[:], in_=tab_s[:].indirect(offsets[:]))
         nc.scalar.dma_start(out=got_s1[0 : P - SHIFT, :].bitcast(I32), in_=got_s[SHIFT:P, :].bitcast(I32))
 
-        late = keep.tile([P, PACK * R + PASSES * PACK * J + 16], F32, name="late", tag="reused", align_bytes=64)
-        for h in range(2):
-            wc_raw[1, h] = load_rows(late[:, h * PACK * half : (h + 1) * PACK * half].rearrange("p (i w) -> p i w", i=PACK), wc, 1, h * half, (h + 1) * half)
-        bias = late[:, PACK * R + PASSES * PACK * J :]
-        with nc.allow_non_contiguous_dma(reason="one bias value to a partition"):
-            nc.sync.dma_start(out=bias[:, 0 : N // P], in_=b.rearrange("(h p) -> p h", p=P))
+        half = R // 2
+        wc_raw = {}
+        for a in range(PASSES):
+            for h in range(2):
+                wc_raw[a, h] = load_rows(wc, a, h * half, (h + 1) * half, "wc_raw%d%d" % (a, h))
         pieces = [(0, 0, 256), (1, 0, 256), (0, 256, 512), (1, 256, 384), (1, 384, 512)]
         c_raw = []
         for a, lo, hi in pieces:
-            at = PACK * (R + a * J)
-            c_raw.append(load_rows(late[:, at + PACK * lo : at + PACK * hi].rearrange("p (i w) -> p i w", i=PACK), c, a, lo, hi))
+            c_raw.append(load_rows(c, a, lo, hi, "c_raw%d_%d" % (a, lo)))
+        for q in range(4):
+            nc.sync.dma_start(out=wd_s[32 * q : 32 * q + 4, :].bitcast(I32), in_=wd_scales[0, 4 * q : 4 * q + 4, :].bitcast(I32))
+        with nc.allow_non_contiguous_dma(reason="one bias value to a partition"):
+            nc.sync.dma_start(out=bias[:], in_=b.rearrange("(h p) -> p h", p=P))
 
         cols = J // 16
         v_q = []
-        got_w = []
-        for g in range(2):
+
+        def look_up(g):
             gw = keep.tile([P, J], I32, name="got_w%d" % g, align_bytes=64)
             nc.vector.tensor_copy(out=gw[:].bitcast(U32), in_=tab_w[:].bitcast(U32).indirect(offsets[:, g * cols : (g + 1) * cols]))
-            got_w.append(gw)
-        for g in range(2):
             vq = keep.tile([P, PASSES, 2 * J], U8, name="v_q%d" % g, align_bytes=64)
-            nc.vector.tensor_copy(out=vq[:].bitcast(U16), in_=got_w[g][:].bitcast(U16).rearrange("p (j d) -> p d j", d=2))
+            nc.vector.tensor_copy(out=vq[:].bitcast(U16), in_=gw[:].bitcast(U16).rearrange("p (j d) -> p d j", d=2))
             v_q.append(vq)
 
-        for a in range(PASSES):
-            nc.vector.tensor_copy(
-                out=w_q[:, a, :].rearrange("p (t c i) -> p c t i", t=4, i=4),
-                in_=w_raw[:, a, :].rearrange("p (c i t) -> p c t i", t=4, i=4),
-            )
-        nc.vector.tensor_copy(
+        look_up(0)
+        nc.gpsimd.tensor_copy(
             out=w_s[:].rearrange("p a (t m) -> p a t m", t=4),
             in_=ws_raw[:].rearrange("p a (m t) -> p a t m", t=4),
         )
+        for a in range(PASSES):
+            nc.gpsimd.tensor_copy(
+                out=w_q[:, a, :].rearrange("p (t c i) -> p c t i", t=4, i=4),
+                in_=w_raw[:, a, :].rearrange("p (c i t) -> p c t i", t=4, i=4),
+            )
+        look_up(1)
 
         wc_q = keep.tile([P, PASSES, R], U32, name="wc_q", align_bytes=64)
         wc_s = keep.tile([P, PASSES, R], U8, name="wc_s", align_bytes=64)
@@ -120,21 +117,44 @@ def tile_list_pnet_bias_kernel(
 
         def wc_pass(a):
             for h in range(2):
-                nc.scalar.copy(
+                move = nc.scalar.copy if h == 0 else nc.vector.tensor_copy
+                move(
                     out=wc_g[a][:, :, h * 64 : (h + 1) * 64, :].rearrange("p t m i -> p m i t"),
-                    in_=wc_raw[a, h].rearrange("p i (m t) -> p m i t", t=4),
+                    in_=wc_raw[a, h][:].rearrange("p i (m t) -> p m i t", t=4),
                 )
             nc.vector.quantize_mx(out=wc_q[:, a, :].bitcast(FP8X4), scales=wc_s[:, a, :], in_=wc_g[a][:].rearrange("p t m i -> p (t m i)"))
 
         wc_pass(0)
         wc_pass(1)
 
-        pooled = keep.tile([P, 4, J], F32, name="pooled")
+        c_q = keep.tile([P, PASSES, J], U32, name="c_q", align_bytes=64)
+        c_s = keep.tile([P, PASSES, J], U8, name="c_s", align_bytes=64)
+        c_g = keep.tile([P, PASSES, J, PACK], BF16, name="c_g", align_bytes=64)
+
+        def c_piece(n):
+            a, lo, hi = pieces[n]
+            dst = c_g[:, a, lo:hi, :].rearrange("p (c j) i -> p c i j", j=4)
+            src = c_raw[n][:].rearrange("p i (c j) -> p c i j", j=4)
+            if n in ON_VECTOR:
+                nc.vector.tensor_copy(out=dst, in_=src)
+            else:
+                nc.scalar.copy(out=dst, in_=src)
+
+        def c_quant(n):
+            a, lo, hi = pieces[n]
+            nc.vector.quantize_mx(out=c_q[:, a, lo:hi].bitcast(FP8X4), scales=c_s[:, a, lo:hi], in_=c_g[:, a, lo:hi, :].rearrange("p j i -> p (j i)"))
+
+        first = keep.tile([P, 4, J], F32, name="first", tag="wc_raw10")
+        pooled = keep.tile([P, 4, J], F32, name="pooled", tag="wc_raw11")
         planes = [got_s, got_s1]
-        for t in range(4):
-            banks = []
-            for g in range(2):
-                bank = psum.tile([P, J], F32, name="nb%d" % g)
+        for g in range(2):
+            if g == 1:
+                c_piece(0)
+                c_piece(1)
+                c_quant(1)
+                c_quant(0)
+            for t in range(4):
+                bank = psum.tile([P, J], F32, name="bank", tag="bank")
                 for a in range(PASSES):
                     nc.tensor.matmul_mx(
                         out=bank[:],
@@ -145,28 +165,19 @@ def tile_list_pnet_bias_kernel(
                         start=(a == 0),
                         stop=(a == PASSES - 1),
                     )
-                banks.append(bank)
-            first = ring.tile([P, J], F32, name="first")
-            nc.scalar.copy(out=first[:], in_=banks[0][:])
-            nc.vector.tensor_tensor(out=pooled[:, t, :], in0=banks[1][:], in1=first[:], op=ALU.max)
+                if g == 0:
+                    nc.scalar.copy(out=first[:, t, :], in_=bank[:])
+                else:
+                    nc.vector.tensor_tensor(out=pooled[:, t, :], in0=bank[:], in1=first[:, t, :], op=ALU.max)
 
-        c_q = keep.tile([P, PASSES, J], U32, name="c_q", align_bytes=64)
-        c_s = keep.tile([P, PASSES, J], U8, name="c_s", align_bytes=64)
-        c_g = keep.tile([P, PASSES, J, PACK], BF16, name="c_g", align_bytes=64)
+        z = keep.tile([P, J, PACK], BF16, name="z", align_bytes=64)
+        hid = keep.tile([P, J * PACK], BF16, name="hid", align_bytes=64)
+        h_q = keep.tile([P, J], U32, name="h_q", align_bytes=64)
+        h_s = keep.tile([P, J], U8, name="h_s", align_bytes=64)
 
-        def c_piece(n):
-            a, lo, hi = pieces[n]
-            dst = c_g[:, a, lo:hi, :].rearrange("p (c j) i -> p c i j", j=4)
-            src = c_raw[n].rearrange("p i (c j) -> p c i j", j=4)
-            if n == len(pieces) - 1:
-                nc.vector.tensor_copy(out=dst, in_=src)
-            else:
-                nc.scalar.copy(out=dst, in_=src)
-            nc.vector.quantize_mx(out=c_q[:, a, lo:hi].bitcast(FP8X4), scales=c_s[:, a, lo:hi], in_=c_g[:, a, lo:hi, :].rearrange("p j i -> p (j i)"))
-
-        def chunk(n):
+        def own_part(n):
             tok = slice(n * CH, (n + 1) * CH)
-            own = psum.tile([P, 4, CH], F32, name="own")
+            own = psum.tile([P, 4, CH], F32, name="own", tag="bank")
             for t in range(4):
                 for a in range(PASSES):
                     nc.tensor.matmul_mx(
@@ -178,40 +189,44 @@ def tile_list_pnet_bias_kernel(
                         start=(a == 0),
                         stop=(a == PASSES - 1),
                     )
-            z = ring.tile([P, CH, PACK], BF16, name="z", align_bytes=64)
             nc.vector.tensor_tensor(
-                out=z[:].rearrange("p (c j) t -> p c t j", j=4),
+                out=z[:, tok, :].rearrange("p (c j) t -> p c t j", j=4),
                 in0=own[:].rearrange("p t (c j) -> p c t j", j=4),
                 in1=pooled[:, :, tok].rearrange("p t (c j) -> p c t j", j=4),
                 op=ALU.add,
             )
-            hid = ring.tile([P, CH * PACK], BF16, name="hid", align_bytes=64)
-            nc.vector.tensor_scalar_max(out=hid[:], in0=z[:].rearrange("p j t -> p (j t)"), scalar1=0.0)
-            h_q = ring.tile([P, CH], U32, name="h_q", align_bytes=64)
-            h_s = ring.tile([P, CH], U8, name="h_s", align_bytes=64)
-            nc.vector.quantize_mx(out=h_q[:].bitcast(FP8X4), scales=h_s[:], in_=hid[:])
-            y = psum.tile([P, N // P, CH], F32, name="y")
-            res = ring.tile([P, N // P, CH], F32, name="res")
+
+        def hidden(lo, hi):
+            nc.vector.tensor_scalar_max(out=hid[:, PACK * lo : PACK * hi], in0=z[:, lo:hi, :].rearrange("p j t -> p (j t)"), scalar1=0.0)
+            nc.vector.quantize_mx(out=h_q[:, lo:hi].bitcast(FP8X4), scales=h_s[:, lo:hi], in_=hid[:, PACK * lo : PACK * hi])
+
+        def second_layer(lo, hi):
+            y = psum.tile([P, N // P, hi - lo], F32, name="y", tag="bank")
+            res = keep.tile([P, N // P, hi - lo], F32, name="res%d" % lo)
             for h in range(N // P):
                 nc.tensor.matmul_mx(
                     out=y[:, h, :],
                     lhsT=wd_q[:, 2 * h * P : 2 * (h + 1) * P].bitcast(FP4X4),
                     lhsT_scale=wd_s[:, h * P : (h + 1) * P],
-                    rhs=h_q[:].bitcast(FP8X4),
-                    rhs_scale=h_s[:],
+                    rhs=h_q[:, lo:hi].bitcast(FP8X4),
+                    rhs_scale=h_s[:, lo:hi],
                     start=True,
                     stop=True,
                 )
             for h in range(N // P):
                 nc.scalar.activation(out=res[:, h, :], in_=y[:, h, :], func=ACT.Identity, bias=bias[:, h : h + 1])
-            nc.sync.dma_start(out=out[:, tok].rearrange("(h p) j -> p h j", p=P), in_=res[:])
+            nc.sync.dma_start(out=out[:, lo:hi].rearrange("(h p) j -> p h j", p=P), in_=res[:])
 
-        c_piece(0)
-        c_piece(1)
-        c_piece(2)
-        chunk(0)
-        c_piece(3)
-        chunk(1)
-        c_piece(4)
-        chunk(2)
-        chunk(3)
+        for n in (2, 3, 4):
+            c_piece(n)
+            c_quant(n)
+        own_part(0)
+        own_part(1)
+        hidden(0, 256)
+        own_part(2)
+        own_part(3)
+        hidden(256, 384)
+        hidden(384, 512)
+        second_layer(0, 256)
+        second_layer(256, 384)
+        second_layer(384, 512)

@@ -22,7 +22,6 @@ KP = P * PACK
 PASSES = K // KP
 CH = 128
 SHIFT = 16
-ON_VECTOR = (1,)
 
 
 def tile_list_pnet_bias_kernel(
@@ -70,20 +69,20 @@ def tile_list_pnet_bias_kernel(
         ws32 = w_scales.bitcast(I32).rearrange("a q r -> q a r")
         for q in range(4):
             nc.sync.dma_start(out=ws_raw[32 * q : 32 * q + 4].bitcast(I32), in_=ws32[4 * q : 4 * q + 4])
-        nc.sync.dma_start(out=w_raw[:], in_=w_words.rearrange("a p r i -> p a (r i)").bitcast(I32))
 
         nc.vector.tensor_copy(out=got_s[:], in_=tab_s[:].indirect(offsets[:]))
-        nc.scalar.dma_start(out=got_s1[0 : P - SHIFT, :].bitcast(I32), in_=got_s[SHIFT:P, :].bitcast(I32))
 
         half = R // 2
-        wc_raw = {}
-        for a in range(PASSES):
-            for h in range(2):
-                wc_raw[a, h] = load_rows(wc, a, h * half, (h + 1) * half, "wc_raw%d%d" % (a, h))
-        pieces = [(0, 0, 256), (1, 0, 256), (0, 256, 512), (1, 256, 384), (1, 384, 512)]
-        c_raw = []
-        for a, lo, hi in pieces:
-            c_raw.append(load_rows(c, a, lo, hi, "c_raw%d_%d" % (a, lo)))
+        wc_whole = load_rows(wc, 0, 0, R, "wc_raw0")
+        nc.sync.dma_start(out=w_raw[:], in_=w_words.rearrange("a p r i -> p a (r i)").bitcast(I32))
+        nc.sync.dma_start(out=got_s1[0 : P - SHIFT, :].bitcast(I32), in_=got_s[SHIFT:P, :].bitcast(I32))
+        wc_raw = {(0, h): wc_whole[:, :, h * half : (h + 1) * half] for h in range(2)}
+        for h in range(2):
+            wc_raw[1, h] = load_rows(wc, 1, h * half, (h + 1) * half, "wc_raw1%d" % h)[:]
+        c_raw = {}
+        for h in range(2):
+            for a in range(PASSES):
+                c_raw[a, h] = load_rows(c, a, h * 256, (h + 1) * 256, "c_raw%d%d" % (a, h))
         for q in range(4):
             nc.sync.dma_start(out=wd_s[32 * q : 32 * q + 4, :].bitcast(I32), in_=wd_scales[0, 4 * q : 4 * q + 4, :].bitcast(I32))
         with nc.allow_non_contiguous_dma(reason="one bias value to a partition"):
@@ -92,24 +91,31 @@ def tile_list_pnet_bias_kernel(
         cols = J // 16
         v_q = []
 
+        got_w = []
+
         def look_up(g):
             gw = keep.tile([P, J], I32, name="got_w%d" % g, align_bytes=64)
             nc.vector.tensor_copy(out=gw[:].bitcast(U32), in_=tab_w[:].bitcast(U32).indirect(offsets[:, g * cols : (g + 1) * cols]))
+            got_w.append(gw)
+
+        def part(g):
             vq = keep.tile([P, PASSES, 2 * J], U8, name="v_q%d" % g, align_bytes=64)
-            nc.vector.tensor_copy(out=vq[:].bitcast(U16), in_=gw[:].bitcast(U16).rearrange("p (j d) -> p d j", d=2))
+            nc.vector.tensor_copy(out=vq[:].bitcast(U16), in_=got_w[g][:].bitcast(U16).rearrange("p (j d) -> p d j", d=2))
             v_q.append(vq)
 
         look_up(0)
-        nc.gpsimd.tensor_copy(
+        nc.vector.tensor_copy(
             out=w_s[:].rearrange("p a (t m) -> p a t m", t=4),
             in_=ws_raw[:].rearrange("p a (m t) -> p a t m", t=4),
         )
+        part(0)
+        look_up(1)
         for a in range(PASSES):
-            nc.gpsimd.tensor_copy(
+            nc.vector.tensor_copy(
                 out=w_q[:, a, :].rearrange("p (t c i) -> p c t i", t=4, i=4),
                 in_=w_raw[:, a, :].rearrange("p (c i t) -> p c t i", t=4, i=4),
             )
-        look_up(1)
+        part(1)
 
         wc_q = keep.tile([P, PASSES, R], U32, name="wc_q", align_bytes=64)
         wc_s = keep.tile([P, PASSES, R], U8, name="wc_s", align_bytes=64)
@@ -117,10 +123,10 @@ def tile_list_pnet_bias_kernel(
 
         def wc_pass(a):
             for h in range(2):
-                move = nc.scalar.copy if h == 0 else nc.vector.tensor_copy
+                move = nc.vector.tensor_copy if (a, h) == (1, 1) else nc.scalar.copy
                 move(
                     out=wc_g[a][:, :, h * 64 : (h + 1) * 64, :].rearrange("p t m i -> p m i t"),
-                    in_=wc_raw[a, h][:].rearrange("p i (m t) -> p m i t", t=4),
+                    in_=wc_raw[a, h].rearrange("p i (m t) -> p m i t", t=4),
                 )
             nc.vector.quantize_mx(out=wc_q[:, a, :].bitcast(FP8X4), scales=wc_s[:, a, :], in_=wc_g[a][:].rearrange("p t m i -> p (t m i)"))
 
@@ -131,44 +137,43 @@ def tile_list_pnet_bias_kernel(
         c_s = keep.tile([P, PASSES, J], U8, name="c_s", align_bytes=64)
         c_g = keep.tile([P, PASSES, J, PACK], BF16, name="c_g", align_bytes=64)
 
-        def c_piece(n):
-            a, lo, hi = pieces[n]
-            dst = c_g[:, a, lo:hi, :].rearrange("p (c j) i -> p c i j", j=4)
-            src = c_raw[n][:].rearrange("p i (c j) -> p c i j", j=4)
-            if n in ON_VECTOR:
-                nc.vector.tensor_copy(out=dst, in_=src)
-            else:
-                nc.scalar.copy(out=dst, in_=src)
-
-        def c_quant(n):
-            a, lo, hi = pieces[n]
+        def c_piece(move, a, lo, hi):
+            at = lo % 256
+            move(
+                out=c_g[:, a, lo:hi, :].rearrange("p (c j) i -> p c i j", j=4),
+                in_=c_raw[a, lo // 256][:, :, at : at + hi - lo].rearrange("p i (c j) -> p c i j", j=4),
+            )
             nc.vector.quantize_mx(out=c_q[:, a, lo:hi].bitcast(FP8X4), scales=c_s[:, a, lo:hi], in_=c_g[:, a, lo:hi, :].rearrange("p j i -> p (j i)"))
 
-        first = keep.tile([P, 4, J], F32, name="first", tag="wc_raw10")
         pooled = keep.tile([P, 4, J], F32, name="pooled", tag="wc_raw11")
         planes = [got_s, got_s1]
-        for g in range(2):
-            if g == 1:
-                c_piece(0)
-                c_piece(1)
-                c_quant(1)
-                c_quant(0)
-            for t in range(4):
-                bank = psum.tile([P, J], F32, name="bank", tag="bank")
-                for a in range(PASSES):
-                    nc.tensor.matmul_mx(
-                        out=bank[:],
-                        lhsT=w_q[:, a, t * P : (t + 1) * P].bitcast(FP8X4),
-                        lhsT_scale=w_s[:, a, t * P : (t + 1) * P],
-                        rhs=v_q[g][:, a, :].bitcast(FP4X4),
-                        rhs_scale=planes[a][:, g * J : (g + 1) * J],
-                        start=(a == 0),
-                        stop=(a == PASSES - 1),
-                    )
-                if g == 0:
-                    nc.scalar.copy(out=first[:, t, :], in_=bank[:])
-                else:
-                    nc.vector.tensor_tensor(out=pooled[:, t, :], in0=bank[:], in1=first[:, t, :], op=ALU.max)
+
+        def neighbour(g, t):
+            bank = psum.tile([P, J], F32, name="bank", tag="bank")
+            for a in range(PASSES):
+                nc.tensor.matmul_mx(
+                    out=bank[:],
+                    lhsT=w_q[:, a, t * P : (t + 1) * P].bitcast(FP8X4),
+                    lhsT_scale=w_s[:, a, t * P : (t + 1) * P],
+                    rhs=v_q[g][:, a, :].bitcast(FP4X4),
+                    rhs_scale=planes[a][:, g * J : (g + 1) * J],
+                    start=(a == 0),
+                    stop=(a == PASSES - 1),
+                )
+            return bank
+
+        banks = [[neighbour(g, t) for g in range(2)] for t in range(4)]
+        first = []
+        for u, slot in enumerate(("wc_raw10", "c_raw00")):
+            if u == 1:
+                c_piece(nc.scalar.copy, 0, 0, 256)
+                c_piece(nc.vector.tensor_copy, 1, 0, 256)
+            pair = keep.tile([P, 2, J], F32, name="first%d" % u, tag=slot)
+            for t in range(2):
+                nc.scalar.copy(out=pair[:, t, :], in_=banks[2 * u + t][0][:])
+                first.append(pair[:, t, :])
+        for t in range(4):
+            nc.vector.tensor_tensor(out=pooled[:, t, :], in0=banks[t][1][:], in1=first[t], op=ALU.max)
 
         z = keep.tile([P, J, PACK], BF16, name="z", align_bytes=64)
         hid = keep.tile([P, J * PACK], BF16, name="hid", align_bytes=64)
@@ -217,9 +222,9 @@ def tile_list_pnet_bias_kernel(
                 nc.scalar.activation(out=res[:, h, :], in_=y[:, h, :], func=ACT.Identity, bias=bias[:, h : h + 1])
             nc.sync.dma_start(out=out[:, lo:hi].rearrange("(h p) j -> p h j", p=P), in_=res[:])
 
-        for n in (2, 3, 4):
-            c_piece(n)
-            c_quant(n)
+        c_piece(nc.scalar.copy, 0, 256, 512)
+        c_piece(nc.scalar.copy, 1, 256, 384)
+        c_piece(nc.scalar.copy, 1, 384, 512)
         own_part(0)
         own_part(1)
         hidden(0, 256)

@@ -162,6 +162,17 @@ def tile_list_pnet_bias_kernel(
                 )
             return bank
 
+        spare = psum.tile([P, J], F32, name="spare", tag="bank")
+        for a in range(PASSES):
+            nc.tensor.matmul_mx(
+                out=spare[:],
+                lhsT=w_raw[:, a, 0:P].bitcast(FP8X4),
+                lhsT_scale=ws_raw[:, a, 0:P],
+                rhs=v_q[0][:, 0, :].bitcast(FP4X4),
+                rhs_scale=got_s[:, 0:J],
+                start=(a == 0),
+                stop=(a == PASSES - 1),
+            )
         banks = [[neighbour(g, t) for g in range(2)] for t in range(4)]
         first = []
         for u, slot in enumerate(("wc_raw10", "c_raw00")):
@@ -175,7 +186,7 @@ def tile_list_pnet_bias_kernel(
         for t in range(4):
             nc.vector.tensor_tensor(out=pooled[:, t, :], in0=banks[t][1][:], in1=first[t], op=ALU.max)
 
-        z = keep.tile([P, J, PACK], BF16, name="z", align_bytes=64)
+        z = [keep.tile([P, CH, PACK], BF16, name="z%d" % n, tag=("c_raw11" if n == 1 else "z%d" % n)) for n in range(4)]
         hid = keep.tile([P, J * PACK], BF16, name="hid", align_bytes=64)
         h_q = keep.tile([P, J], U32, name="h_q", align_bytes=64)
         h_s = keep.tile([P, J], U8, name="h_s", align_bytes=64)
@@ -195,22 +206,29 @@ def tile_list_pnet_bias_kernel(
                         stop=(a == PASSES - 1),
                     )
             nc.vector.tensor_tensor(
-                out=z[:, tok, :].rearrange("p (c j) t -> p c t j", j=4),
+                out=z[n][:].rearrange("p (c j) t -> p c t j", j=4),
                 in0=own[:].rearrange("p t (c j) -> p c t j", j=4),
                 in1=pooled[:, :, tok].rearrange("p t (c j) -> p c t j", j=4),
                 op=ALU.add,
             )
 
-        def hidden(lo, hi):
-            nc.vector.tensor_scalar_max(out=hid[:, PACK * lo : PACK * hi], in0=z[:, lo:hi, :].rearrange("p j t -> p (j t)"), scalar1=0.0)
+        def relu(n):
+            src = z[n][:].rearrange("p j t -> p (j t)")
+            dst = hid[:, PACK * CH * n : PACK * CH * (n + 1)]
+            if n < 3:
+                nc.scalar.activation(out=dst, in_=src, func=ACT.Relu)
+            else:
+                nc.vector.tensor_scalar_max(out=dst, in0=src, scalar1=0.0)
+
+        def h_quant(lo, hi):
             nc.vector.quantize_mx(out=h_q[:, lo:hi].bitcast(FP8X4), scales=h_s[:, lo:hi], in_=hid[:, PACK * lo : PACK * hi])
 
-        def second_layer(lo, hi):
-            y = psum.tile([P, N // P, hi - lo], F32, name="y", tag="bank")
-            res = keep.tile([P, N // P, hi - lo], F32, name="res%d" % lo)
+        def second_layer(lo, hi, both_engines):
             for h in range(N // P):
+                y = psum.tile([P, hi - lo], F32, name="y", tag="bank")
+                res = keep.tile([P, hi - lo], F32, name="res%d_%d" % (lo, h))
                 nc.tensor.matmul_mx(
-                    out=y[:, h, :],
+                    out=y[:],
                     lhsT=wd_q[:, 2 * h * P : 2 * (h + 1) * P].bitcast(FP4X4),
                     lhsT_scale=wd_s[:, h * P : (h + 1) * P],
                     rhs=h_q[:, lo:hi].bitcast(FP8X4),
@@ -218,20 +236,22 @@ def tile_list_pnet_bias_kernel(
                     start=True,
                     stop=True,
                 )
-            for h in range(N // P):
-                nc.scalar.activation(out=res[:, h, :], in_=y[:, h, :], func=ACT.Identity, bias=bias[:, h : h + 1])
-            nc.sync.dma_start(out=out[:, lo:hi].rearrange("(h p) j -> p h j", p=P), in_=res[:])
+                if both_engines and h == 1:
+                    nc.vector.tensor_scalar_add(out=res[:], in0=y[:], scalar1=bias[:, h : h + 1])
+                else:
+                    nc.scalar.activation(out=res[:], in_=y[:], func=ACT.Identity, bias=bias[:, h : h + 1])
+                nc.sync.dma_start(out=out[h * P : (h + 1) * P, lo:hi], in_=res[:])
 
         c_piece(nc.scalar.copy, 0, 256, 512)
         c_piece(nc.scalar.copy, 1, 256, 384)
         c_piece(nc.scalar.copy, 1, 384, 512)
-        own_part(0)
-        own_part(1)
-        hidden(0, 256)
-        own_part(2)
-        own_part(3)
-        hidden(256, 384)
-        hidden(384, 512)
-        second_layer(0, 256)
-        second_layer(256, 384)
-        second_layer(384, 512)
+        for n in range(4):
+            own_part(n)
+        for n in range(4):
+            relu(n)
+        h_quant(0, 256)
+        h_quant(256, 384)
+        h_quant(384, 512)
+        second_layer(0, 256, False)
+        second_layer(256, 384, True)
+        second_layer(384, 512, True)

@@ -30,7 +30,7 @@ def tile_list_pnet_bias_kernel(
     nc = tc.nc
     with ExitStack() as ctx:
         keep = ctx.enter_context(tc.tile_pool(name="keep", bufs=1))
-        psum = ctx.enter_context(tc.psum_pool(name="psum", bufs=8))
+        psum = ctx.enter_context(tc.psum_pool(name="psum", bufs=1))
 
         offsets = keep.tile([P, 2 * J // 16], U16, name="offsets")
         tab_s = keep.tile([P, T], U8, name="tab_s", align_bytes=64)
@@ -62,7 +62,7 @@ def tile_list_pnet_bias_kernel(
         nc.sync.dma_start(out=tab_w[:], in_=tab_words[0].rearrange("p t b -> p (t b)").bitcast(I32))
 
         def load_rows(src, a, lo, hi, name):
-            raw = keep.tile([P, PACK, hi - lo], F32, name=name, tag=name)
+            raw = keep.tile([P, PACK, hi - lo], F32, name=name, tag=name, align_bytes=64)
             nc.sync.dma_start(out=raw[:], in_=src[a * KP : (a + 1) * KP, lo:hi].rearrange("(p i) w -> p i w", i=PACK))
             return raw
 
@@ -119,7 +119,7 @@ def tile_list_pnet_bias_kernel(
 
         wc_q = keep.tile([P, PASSES, R], U32, name="wc_q", align_bytes=64)
         wc_s = keep.tile([P, PASSES, R], U8, name="wc_s", align_bytes=64)
-        wc_g = [keep.tile([P, 4, P, PACK], BF16, name="wc_g%d" % a, align_bytes=64) for a in range(PASSES)]
+        wc_g = [keep.tile([P, 4, P, PACK], BF16, name="wc_g%d" % a, tag="wc_g%d" % a, align_bytes=64) for a in range(PASSES)]
 
         def wc_pass(a):
             for h in range(2):
@@ -145,11 +145,11 @@ def tile_list_pnet_bias_kernel(
             )
             nc.vector.quantize_mx(out=c_q[:, a, lo:hi].bitcast(FP8X4), scales=c_s[:, a, lo:hi], in_=c_g[:, a, lo:hi, :].rearrange("p j i -> p (j i)"))
 
-        pooled = keep.tile([P, 4, J], F32, name="pooled", tag="wc_raw11")
+        pooled = keep.tile([P, 4, J], F32, name="pooled", tag="wc_raw11", align_bytes=64)
         planes = [got_s, got_s1]
 
-        def neighbour(g, t):
-            bank = psum.tile([P, J], F32, name="bank", tag="bank")
+        def neighbour(g, t, slot):
+            bank = psum.tile([P, J], F32, name="a%d_%d" % (g, t), tag="bank%d" % slot)
             for a in range(PASSES):
                 nc.tensor.matmul_mx(
                     out=bank[:],
@@ -162,7 +162,7 @@ def tile_list_pnet_bias_kernel(
                 )
             return bank
 
-        spare = psum.tile([P, J], F32, name="spare", tag="bank")
+        spare = psum.tile([P, J], F32, name="spare", tag="bank7")
         for a in range(PASSES):
             nc.tensor.matmul_mx(
                 out=spare[:],
@@ -173,38 +173,56 @@ def tile_list_pnet_bias_kernel(
                 start=(a == 0),
                 stop=(a == PASSES - 1),
             )
-        banks = [[neighbour(g, t) for g in range(2)] for t in range(4)]
-        first = []
-        for u, slot in enumerate(("wc_raw10", "c_raw00")):
-            if u == 1:
-                c_piece(nc.scalar.copy, 0, 0, 256)
-                c_piece(nc.vector.tensor_copy, 1, 0, 256)
-            pair = keep.tile([P, 2, J], F32, name="first%d" % u, tag=slot)
-            for t in range(2):
-                nc.scalar.copy(out=pair[:, t, :], in_=banks[2 * u + t][0][:])
-                first.append(pair[:, t, :])
-        for t in range(4):
+        banks = [{0: neighbour(0, t, t)} for t in range(4)]
+        for t in range(3):
+            banks[t][1] = neighbour(1, t, 4 + t)
+        early = keep.tile([P, 3, J], F32, name="first_early", tag="wc_raw10", align_bytes=64)
+        first = [early[:, t, :] for t in range(3)]
+        for t in range(3):
+            nc.scalar.copy(out=first[t], in_=banks[t][0][:])
+
+        def pool(t):
             nc.vector.tensor_tensor(out=pooled[:, t, :], in0=banks[t][1][:], in1=first[t], op=ALU.max)
 
-        z = [keep.tile([P, CH, PACK], BF16, name="z%d" % n, tag=("c_raw11" if n == 1 else "z%d" % n)) for n in range(4)]
-        hid = keep.tile([P, J * PACK], BF16, name="hid", align_bytes=64)
+        pool(0)
+        pool(1)
+        banks[3][1] = neighbour(1, 3, 5)
+        pool(2)
+        c_g00 = keep.tile([P, 256, PACK], BF16, name="c_g00", tag="wc_g1", align_bytes=64)
+        nc.gpsimd.tensor_scalar(out=c_g00[:], in0=c_raw[0, 0][:].rearrange("p i j -> p j i"), scalar1=1.0, scalar2=0.0, op0=ALU.mult, op1=ALU.add)
+        nc.vector.quantize_mx(out=c_q[:, 0, 0:256].bitcast(FP8X4), scales=c_s[:, 0, 0:256], in_=c_g00[:].rearrange("p j i -> p (j i)"))
+        c_piece(nc.scalar.copy, 1, 0, 256)
+        late = keep.tile([P, J], F32, name="first_late", tag="c_raw10", align_bytes=64)
+        first.append(late[:])
+        nc.scalar.copy(out=first[3], in_=banks[3][0][:])
+        pool(3)
+
+        z = {}
+        hid = keep.tile([P, J * PACK], BF16, name="hid", tag="c_raw11", align_bytes=64)
         h_q = keep.tile([P, J], U32, name="h_q", align_bytes=64)
         h_s = keep.tile([P, J], U8, name="h_s", align_bytes=64)
 
+        owns = {}
+
+        def own_pass(n, a):
+            tok = slice(n * CH, (n + 1) * CH)
+            if a == 0:
+                owns[n] = psum.tile([P, 4, CH], F32, name="own%d" % n, tag="bank%d" % n)
+            for t in range(4):
+                nc.tensor.matmul_mx(
+                    out=owns[n][:, t, :],
+                    lhsT=wc_q[:, a, t * P : (t + 1) * P].bitcast(FP8X4),
+                    lhsT_scale=wc_s[:, a, t * P : (t + 1) * P],
+                    rhs=c_q[:, a, tok].bitcast(FP8X4),
+                    rhs_scale=c_s[:, a, tok],
+                    start=(a == 0 and t == 0),
+                    stop=(a == PASSES - 1 and t == 3),
+                )
+
         def own_part(n):
             tok = slice(n * CH, (n + 1) * CH)
-            own = psum.tile([P, 4, CH], F32, name="own", tag="bank")
-            for t in range(4):
-                for a in range(PASSES):
-                    nc.tensor.matmul_mx(
-                        out=own[:, t, :],
-                        lhsT=wc_q[:, a, t * P : (t + 1) * P].bitcast(FP8X4),
-                        lhsT_scale=wc_s[:, a, t * P : (t + 1) * P],
-                        rhs=c_q[:, a, tok].bitcast(FP8X4),
-                        rhs_scale=c_s[:, a, tok],
-                        start=(a == 0),
-                        stop=(a == PASSES - 1),
-                    )
+            own = owns[n]
+            z[n] = keep.tile([P, CH, PACK], BF16, name="z%d" % n, tag=("c_g01" if n == 1 else "z%d" % n), align_bytes=64)
             nc.vector.tensor_tensor(
                 out=z[n][:].rearrange("p (c j) t -> p c t j", j=4),
                 in0=own[:].rearrange("p t (c j) -> p c t j", j=4),
@@ -225,7 +243,7 @@ def tile_list_pnet_bias_kernel(
 
         def second_layer(lo, hi, both_engines):
             for h in range(N // P):
-                y = psum.tile([P, hi - lo], F32, name="y", tag="bank")
+                y = psum.tile([P, hi - lo], F32, name="y%d_%d" % (lo, h), tag="bank%d" % {0: (7, 4), 256: (6, 5), 384: (0, 1)}[lo][h])
                 res = keep.tile([P, hi - lo], F32, name="res%d_%d" % (lo, h))
                 nc.tensor.matmul_mx(
                     out=y[:],
@@ -242,9 +260,18 @@ def tile_list_pnet_bias_kernel(
                     nc.scalar.activation(out=res[:], in_=y[:], func=ACT.Identity, bias=bias[:, h : h + 1])
                 nc.sync.dma_start(out=out[h * P : (h + 1) * P, lo:hi], in_=res[:])
 
-        c_piece(nc.scalar.copy, 0, 256, 512)
-        c_piece(nc.scalar.copy, 1, 256, 384)
-        c_piece(nc.scalar.copy, 1, 384, 512)
+        for n in range(2):
+            own_pass(n, 0)
+        for n in range(2):
+            own_pass(n, 1)
+        c_g01 = keep.tile([P, 256, PACK], BF16, name="c_g01", tag="c_g01", align_bytes=64)
+        nc.scalar.copy(out=c_g01[:].rearrange("p (c j) i -> p c i j", j=4), in_=c_raw[0, 1][:].rearrange("p i (c j) -> p c i j", j=4))
+        nc.vector.quantize_mx(out=c_q[:, 0, 256:512].bitcast(FP8X4), scales=c_s[:, 0, 256:512], in_=c_g01[:].rearrange("p j i -> p (j i)"))
+        own_pass(2, 0)
+        own_pass(3, 0)
+        for n in (2, 3):
+            c_piece(nc.scalar.copy, 1, n * CH, (n + 1) * CH)
+            own_pass(n, 1)
         for n in range(4):
             own_part(n)
         for n in range(4):
@@ -252,6 +279,6 @@ def tile_list_pnet_bias_kernel(
         h_quant(0, 256)
         h_quant(256, 384)
         h_quant(384, 512)
-        second_layer(0, 256, False)
+        second_layer(0, 256, True)
         second_layer(256, 384, True)
         second_layer(384, 512, True)

@@ -44,11 +44,8 @@ def tile_list_pnet_bias_kernel(
         wd_q = keep.tile([P, 2 * N], U8, name="wd_q", align_bytes=64)
         wd_s = keep.tile([P, N], U8, name="wd_s", align_bytes=64)
         bias = keep.tile([P, N // P], F32, name="bias")
-        warm_in = keep.tile([P, 8], F32, name="warm_in")
-        warm_out = keep.tile([P, 8], F32, name="warm_out")
 
         nc.gpsimd.memset(tab_s[:].bitcast(I32), 0)
-        nc.gpsimd.memset(warm_in[:], 0.0)
         nc.vector.memset(ws_raw[:].rearrange("p a r -> p (a r)").bitcast(I32), 0)
         nc.vector.memset(wd_s[:].bitcast(I32), 0)
         nc.vector.memset(got_s1[:].bitcast(I32), 0)
@@ -58,7 +55,6 @@ def tile_list_pnet_bias_kernel(
         ts32 = tab_scales.bitcast(I32).rearrange("a (q r) t -> r q a t", r=4)
         for r in range(4):
             nc.sync.dma_start(out=tab_s[r:P:SHIFT, :].bitcast(I32), in_=ts32[r])
-        nc.scalar.activation(out=warm_out[:], in_=warm_in[:], func=ACT.Identity, bias=warm_in[:, 0:1])
         nc.sync.dma_start(out=tab_w[:], in_=tab_words[0].rearrange("p t b -> p (t b)").bitcast(I32))
 
         def load_rows(src, a, lo, hi, name):
@@ -162,17 +158,6 @@ def tile_list_pnet_bias_kernel(
                 )
             return bank
 
-        spare = psum.tile([P, J], F32, name="spare", tag="bank7")
-        for a in range(PASSES):
-            nc.tensor.matmul_mx(
-                out=spare[:],
-                lhsT=w_raw[:, a, 0:P].bitcast(FP8X4),
-                lhsT_scale=ws_raw[:, a, 0:P],
-                rhs=v_q[0][:, 0, :].bitcast(FP4X4),
-                rhs_scale=got_s[:, 0:J],
-                start=(a == 0),
-                stop=(a == PASSES - 1),
-            )
         banks = [{0: neighbour(0, t, t)} for t in range(4)]
         for t in range(3):
             banks[t][1] = neighbour(1, t, 4 + t)

@@ -45,12 +45,14 @@ def tile_list_pnet_bias_kernel(
         wd_s = keep.tile([P, N], U8, name="wd_s", align_bytes=64)
         bias = keep.tile([P, N // P], F32, name="bias")
 
-        nc.gpsimd.memset(tab_s[:].bitcast(I32), 0)
-        nc.vector.memset(ws_raw[:].rearrange("p a r -> p (a r)").bitcast(I32), 0)
+        nc.gpsimd.memset(ws_raw[:].rearrange("p a r -> p (a r)").bitcast(I32), 0)
+        nc.gpsimd.memset(tab_s[:, 0 : T // 2].bitcast(I32), 0)
+        nc.vector.memset(tab_s[:, T // 2 : T].bitcast(I32), 0)
         nc.vector.memset(wd_s[:].bitcast(I32), 0)
         nc.vector.memset(got_s1[:].bitcast(I32), 0)
 
         nc.sync.dma_start(offsets[:], offs)
+        nc.sync.dma_start(out=ws_raw[0:16].bitcast(I32), in_=w_scales.bitcast(I32).rearrange("a q r -> q a r"))
         nc.sync.dma_start(out=wd_q[:].bitcast(I32), in_=wd_words[0].bitcast(I32))
         ts32 = tab_scales.bitcast(I32).rearrange("a (q r) t -> r q a t", r=4)
         for r in range(4):
@@ -62,9 +64,12 @@ def tile_list_pnet_bias_kernel(
             nc.sync.dma_start(out=raw[:], in_=src[a * KP : (a + 1) * KP, lo:hi].rearrange("(p i) w -> p i w", i=PACK))
             return raw
 
-        ws32 = w_scales.bitcast(I32).rearrange("a q r -> q a r")
-        for q in range(4):
-            nc.sync.dma_start(out=ws_raw[32 * q : 32 * q + 4].bitcast(I32), in_=ws32[4 * q : 4 * q + 4])
+        nc.vector.tensor_copy(
+            out=w_s[:].rearrange("p a (t m) -> p a t m", t=4),
+            in_=ws_raw[:].rearrange("p a (m t) -> p a t m", t=4),
+        )
+        for q in range(1, 4):
+            nc.sync.dma_start(out=w_s[32 * q : 32 * q + 4].bitcast(I32), in_=w_s[4 * q : 4 * q + 4].bitcast(I32))
 
         nc.vector.tensor_copy(out=got_s[:], in_=tab_s[:].indirect(offsets[:]))
 
@@ -100,10 +105,6 @@ def tile_list_pnet_bias_kernel(
             v_q.append(vq)
 
         look_up(0)
-        nc.vector.tensor_copy(
-            out=w_s[:].rearrange("p a (t m) -> p a t m", t=4),
-            in_=ws_raw[:].rearrange("p a (m t) -> p a t m", t=4),
-        )
         part(0)
         look_up(1)
         for a in range(PASSES):

@@ -37,7 +37,7 @@ def tile_list_pnet_bias_kernel(
         tab_w = keep.tile([P, T], I32, name="tab_w", align_bytes=64)
         got_s = keep.tile([P, 2 * J], U8, name="got_s", align_bytes=64)
         got_s1 = keep.tile([P, 2 * J], U8, name="got_s1", align_bytes=64)
-        w_raw = keep.tile([P, PASSES, R], I32, name="w_raw", align_bytes=64)
+        w_raw = [keep.tile([P, R], I32, name="w_raw%d" % a, tag="w_raw%d" % a, align_bytes=64) for a in range(PASSES)]
         ws_raw = keep.tile([P, PASSES, R], U8, name="ws_raw", align_bytes=64)
         w_q = keep.tile([P, PASSES, R], I32, name="w_q", align_bytes=64)
         w_s = keep.tile([P, PASSES, R], U8, name="w_s", align_bytes=64)
@@ -53,7 +53,11 @@ def tile_list_pnet_bias_kernel(
 
         nc.sync.dma_start(offsets[:], offs)
         nc.sync.dma_start(out=ws_raw[0:16].bitcast(I32), in_=w_scales.bitcast(I32).rearrange("a q r -> q a r"))
-        nc.sync.dma_start(out=wd_q[:].bitcast(I32), in_=wd_words[0].bitcast(I32))
+
+        def load_w(a):
+            nc.sync.dma_start(out=w_raw[a][:], in_=w_words[a].rearrange("p r i -> p (r i)").bitcast(I32))
+
+        load_w(0)
         ts32 = tab_scales.bitcast(I32).rearrange("a (q r) t -> r q a t", r=4)
         for r in range(4):
             nc.sync.dma_start(out=tab_s[r:P:SHIFT, :].bitcast(I32), in_=ts32[r])
@@ -68,14 +72,14 @@ def tile_list_pnet_bias_kernel(
             out=w_s[:].rearrange("p a (t m) -> p a t m", t=4),
             in_=ws_raw[:].rearrange("p a (m t) -> p a t m", t=4),
         )
-        for q in range(1, 4):
-            nc.sync.dma_start(out=w_s[32 * q : 32 * q + 4].bitcast(I32), in_=w_s[4 * q : 4 * q + 4].bitcast(I32))
-
         nc.vector.tensor_copy(out=got_s[:], in_=tab_s[:].indirect(offsets[:]))
 
         half = R // 2
         wc_whole = load_rows(wc, 0, 0, R, "wc_raw0")
-        nc.sync.dma_start(out=w_raw[:], in_=w_words.rearrange("a p r i -> p a (r i)").bitcast(I32))
+        load_w(1)
+        for q in range(1, 4):
+            nc.sync.dma_start(out=w_s[32 * q : 32 * q + 4].bitcast(I32), in_=w_s[4 * q : 4 * q + 4].bitcast(I32))
+
         nc.sync.dma_start(out=got_s1[0 : P - SHIFT, :].bitcast(I32), in_=got_s[SHIFT:P, :].bitcast(I32))
         wc_raw = {(0, h): wc_whole[:, :, h * half : (h + 1) * half] for h in range(2)}
         for h in range(2):
@@ -84,6 +88,7 @@ def tile_list_pnet_bias_kernel(
         for h in range(2):
             for a in range(PASSES):
                 c_raw[a, h] = load_rows(c, a, h * 256, (h + 1) * 256, "c_raw%d%d" % (a, h))
+        nc.sync.dma_start(out=wd_q[:].bitcast(I32), in_=wd_words[0].bitcast(I32))
         for q in range(4):
             nc.sync.dma_start(out=wd_s[32 * q : 32 * q + 4, :].bitcast(I32), in_=wd_scales[0, 4 * q : 4 * q + 4, :].bitcast(I32))
         with nc.allow_non_contiguous_dma(reason="one bias value to a partition"):
@@ -100,7 +105,7 @@ def tile_list_pnet_bias_kernel(
             got_w.append(gw)
 
         def part(g):
-            vq = keep.tile([P, PASSES, 2 * J], U8, name="v_q%d" % g, align_bytes=64)
+            vq = keep.tile([P, PASSES, 2 * J], U8, name="v_q%d" % g, tag=("v_q0", "w_raw1")[g], align_bytes=64)
             nc.vector.tensor_copy(out=vq[:].bitcast(U16), in_=got_w[g][:].bitcast(U16).rearrange("p (j d) -> p d j", d=2))
             v_q.append(vq)
 
@@ -110,7 +115,7 @@ def tile_list_pnet_bias_kernel(
         for a in range(PASSES):
             nc.vector.tensor_copy(
                 out=w_q[:, a, :].rearrange("p (t c i) -> p c t i", t=4, i=4),
-                in_=w_raw[:, a, :].rearrange("p (c i t) -> p c t i", t=4, i=4),
+                in_=w_raw[a][:].rearrange("p (c i t) -> p c t i", t=4, i=4),
             )
         part(1)
 
@@ -118,17 +123,23 @@ def tile_list_pnet_bias_kernel(
         wc_s = keep.tile([P, PASSES, R], U8, name="wc_s", align_bytes=64)
         wc_g = [keep.tile([P, 4, P, PACK], BF16, name="wc_g%d" % a, tag="wc_g%d" % a, align_bytes=64) for a in range(PASSES)]
 
-        def wc_pass(a):
-            for h in range(2):
-                move = nc.vector.tensor_copy if (a, h) == (1, 1) else nc.scalar.copy
-                move(
-                    out=wc_g[a][:, :, h * 64 : (h + 1) * 64, :].rearrange("p t m i -> p m i t"),
-                    in_=wc_raw[a, h].rearrange("p i (m t) -> p m i t", t=4),
-                )
+        def wc_cast(move, a, lo, hi):
+            at = lo % half
+            move(
+                out=wc_g[a][:, :, lo // 4 : hi // 4, :].rearrange("p t m i -> p m i t"),
+                in_=wc_raw[a, lo // half][:, :, at : at + hi - lo].rearrange("p i (m t) -> p m i t", t=4),
+            )
+
+        def wc_quant(a):
             nc.vector.quantize_mx(out=wc_q[:, a, :].bitcast(FP8X4), scales=wc_s[:, a, :], in_=wc_g[a][:].rearrange("p t m i -> p (t m i)"))
 
-        wc_pass(0)
-        wc_pass(1)
+        wc_cast(nc.scalar.copy, 0, 0, half)
+        wc_cast(nc.scalar.copy, 0, half, R)
+        wc_cast(nc.scalar.copy, 1, 0, 128)
+        wc_cast(nc.vector.tensor_copy, 1, 128, half)
+        wc_cast(nc.vector.tensor_copy, 1, half, R)
+        wc_quant(0)
+        wc_quant(1)
 
         c_q = keep.tile([P, PASSES, J], U32, name="c_q", align_bytes=64)
         c_s = keep.tile([P, PASSES, J], U8, name="c_s", align_bytes=64)
@@ -256,7 +267,7 @@ def tile_list_pnet_bias_kernel(
         own_pass(2, 0)
         own_pass(3, 0)
         for n in (2, 3):
-            c_piece(nc.scalar.copy, 1, n * CH, (n + 1) * CH)
+            c_piece(nc.scalar.copy if n == 2 else nc.vector.tensor_copy, 1, n * CH, (n + 1) * CH)
             own_pass(n, 1)
         for n in range(4):
             own_part(n)

@@ -33,16 +33,16 @@ def tile_list_pnet_bias_kernel(
         psum = ctx.enter_context(tc.psum_pool(name="psum", bufs=1))
 
         offsets = keep.tile([P, 2 * J // 16], U16, name="offsets")
-        tab_s = keep.tile([P, T], U8, name="tab_s", align_bytes=64)
-        tab_w = keep.tile([P, T], I32, name="tab_w", align_bytes=64)
-        got_s = keep.tile([P, 2 * J], U8, name="got_s", align_bytes=64)
-        got_s1 = keep.tile([P, 2 * J], U8, name="got_s1", align_bytes=64)
-        w_raw = [keep.tile([P, R], I32, name="w_raw%d" % a, tag="w_raw%d" % a, align_bytes=64) for a in range(PASSES)]
-        ws_raw = keep.tile([P, PASSES, R], U8, name="ws_raw", align_bytes=64)
-        w_q = keep.tile([P, PASSES, R], I32, name="w_q", align_bytes=64)
-        w_s = keep.tile([P, PASSES, R], U8, name="w_s", align_bytes=64)
-        wd_q = keep.tile([P, 2 * N], U8, name="wd_q", align_bytes=64)
-        wd_s = keep.tile([P, N], U8, name="wd_s", align_bytes=64)
+        tab_s = keep.tile([P, T], U8, name="tab_s", align_bytes=256)
+        tab_w = keep.tile([P, T], I32, name="tab_w", align_bytes=256)
+        got_s = keep.tile([P, 2 * J], U8, name="got_s", align_bytes=256)
+        got_s1 = keep.tile([P, 2 * J], U8, name="got_s1", align_bytes=256)
+        w_raw = [keep.tile([P, R], I32, name="w_raw%d" % a, tag="w_raw%d" % a, align_bytes=256) for a in range(PASSES)]
+        ws_raw = keep.tile([P, PASSES, R], U8, name="ws_raw", align_bytes=256)
+        w_q = keep.tile([P, PASSES, R], I32, name="w_q", align_bytes=256)
+        w_s = keep.tile([P, PASSES, R], U8, name="w_s", align_bytes=256)
+        wd_q = keep.tile([P, 2 * N], U8, name="wd_q", align_bytes=256)
+        wd_s = keep.tile([P, N], U8, name="wd_s", align_bytes=256)
         bias = keep.tile([P, N // P], F32, name="bias")
 
         nc.gpsimd.memset(ws_raw[:].rearrange("p a r -> p (a r)").bitcast(I32), 0)
@@ -64,7 +64,7 @@ def tile_list_pnet_bias_kernel(
         nc.sync.dma_start(out=tab_w[:], in_=tab_words[0].rearrange("p t b -> p (t b)").bitcast(I32))
 
         def load_rows(src, a, lo, hi, name):
-            raw = keep.tile([P, PACK, hi - lo], F32, name=name, tag=name, align_bytes=64)
+            raw = keep.tile([P, PACK, hi - lo], F32, name=name, tag=name, align_bytes=256)
             nc.sync.dma_start(out=raw[:], in_=src[a * KP : (a + 1) * KP, lo:hi].rearrange("(p i) w -> p i w", i=PACK))
             return raw
 
@@ -100,12 +100,12 @@ def tile_list_pnet_bias_kernel(
         got_w = []
 
         def look_up(g):
-            gw = keep.tile([P, J], I32, name="got_w%d" % g, align_bytes=64)
+            gw = keep.tile([P, J], I32, name="got_w%d" % g, align_bytes=256)
             nc.vector.tensor_copy(out=gw[:].bitcast(U32), in_=tab_w[:].bitcast(U32).indirect(offsets[:, g * cols : (g + 1) * cols]))
             got_w.append(gw)
 
         def part(g):
-            vq = keep.tile([P, PASSES, 2 * J], U8, name="v_q%d" % g, tag=("v_q0", "w_raw1")[g], align_bytes=64)
+            vq = keep.tile([P, PASSES, 2 * J], U8, name="v_q%d" % g, tag=("v_q0", "w_raw1")[g], align_bytes=256)
             nc.vector.tensor_copy(out=vq[:].bitcast(U16), in_=got_w[g][:].bitcast(U16).rearrange("p (j d) -> p d j", d=2))
             v_q.append(vq)
 
@@ -119,9 +119,9 @@ def tile_list_pnet_bias_kernel(
             )
         part(1)
 
-        wc_q = keep.tile([P, PASSES, R], U32, name="wc_q", align_bytes=64)
-        wc_s = keep.tile([P, PASSES, R], U8, name="wc_s", align_bytes=64)
-        wc_g = [keep.tile([P, 4, P, PACK], BF16, name="wc_g%d" % a, tag="wc_g%d" % a, align_bytes=64) for a in range(PASSES)]
+        wc_q = keep.tile([P, PASSES, R], U32, name="wc_q", align_bytes=256)
+        wc_s = keep.tile([P, PASSES, R], U8, name="wc_s", align_bytes=256)
+        wc_g = [keep.tile([P, 4, P, PACK], BF16, name="wc_g%d" % a, tag="wc_g%d" % a, align_bytes=256) for a in range(PASSES)]
 
         def wc_cast(move, a, lo, hi):
             at = lo % half
@@ -141,9 +141,9 @@ def tile_list_pnet_bias_kernel(
         wc_quant(0)
         wc_quant(1)
 
-        c_q = keep.tile([P, PASSES, J], U32, name="c_q", align_bytes=64)
-        c_s = keep.tile([P, PASSES, J], U8, name="c_s", align_bytes=64)
-        c_g = keep.tile([P, PASSES, J, PACK], BF16, name="c_g", align_bytes=64)
+        c_q = keep.tile([P, PASSES, J], U32, name="c_q", align_bytes=256)
+        c_s = keep.tile([P, PASSES, J], U8, name="c_s", align_bytes=256)
+        c_g = keep.tile([P, PASSES, J, PACK], BF16, name="c_g", align_bytes=256)
 
         def c_piece(move, a, lo, hi):
             at = lo % 256
@@ -153,7 +153,7 @@ def tile_list_pnet_bias_kernel(
             )
             nc.vector.quantize_mx(out=c_q[:, a, lo:hi].bitcast(FP8X4), scales=c_s[:, a, lo:hi], in_=c_g[:, a, lo:hi, :].rearrange("p j i -> p (j i)"))
 
-        pooled = keep.tile([P, 4, J], F32, name="pooled", tag="wc_raw11", align_bytes=64)
+        pooled = keep.tile([P, 4, J], F32, name="pooled", tag="wc_raw11", align_bytes=256)
         planes = [got_s, got_s1]
 
         def neighbour(g, t, slot):
@@ -173,7 +173,7 @@ def tile_list_pnet_bias_kernel(
         banks = [{0: neighbour(0, t, t)} for t in range(4)]
         for t in range(3):
             banks[t][1] = neighbour(1, t, 4 + t)
-        early = keep.tile([P, 3, J], F32, name="first_early", tag="wc_raw10", align_bytes=64)
+        early = keep.tile([P, 3, J], F32, name="first_early", tag="wc_raw10", align_bytes=256)
         first = [early[:, t, :] for t in range(3)]
         for t in range(3):
             nc.scalar.copy(out=first[t], in_=banks[t][0][:])
@@ -185,19 +185,19 @@ def tile_list_pnet_bias_kernel(
         pool(1)
         banks[3][1] = neighbour(1, 3, 5)
         pool(2)
-        c_g00 = keep.tile([P, 256, PACK], BF16, name="c_g00", tag="wc_g1", align_bytes=64)
+        c_g00 = keep.tile([P, 256, PACK], BF16, name="c_g00", tag="wc_g1", align_bytes=256)
         nc.gpsimd.tensor_scalar(out=c_g00[:], in0=c_raw[0, 0][:].rearrange("p i j -> p j i"), scalar1=1.0, scalar2=0.0, op0=ALU.mult, op1=ALU.add)
         nc.vector.quantize_mx(out=c_q[:, 0, 0:256].bitcast(FP8X4), scales=c_s[:, 0, 0:256], in_=c_g00[:].rearrange("p j i -> p (j i)"))
         c_piece(nc.scalar.copy, 1, 0, 256)
-        late = keep.tile([P, J], F32, name="first_late", tag="c_raw10", align_bytes=64)
+        late = keep.tile([P, J], F32, name="first_late", tag="c_raw10", align_bytes=256)
         first.append(late[:])
         nc.scalar.copy(out=first[3], in_=banks[3][0][:])
         pool(3)
 
         z = {}
-        hid = keep.tile([P, J * PACK], BF16, name="hid", tag="c_raw11", align_bytes=64)
-        h_q = keep.tile([P, J], U32, name="h_q", align_bytes=64)
-        h_s = keep.tile([P, J], U8, name="h_s", align_bytes=64)
+        hid = keep.tile([P, J * PACK], BF16, name="hid", tag="c_raw11", align_bytes=256)
+        h_q = keep.tile([P, J], U32, name="h_q", align_bytes=256)
+        h_s = keep.tile([P, J], U8, name="h_s", align_bytes=256)
 
         owns = {}
 
@@ -219,7 +219,7 @@ def tile_list_pnet_bias_kernel(
         def own_part(n):
             tok = slice(n * CH, (n + 1) * CH)
             own = owns[n]
-            z[n] = keep.tile([P, CH, PACK], BF16, name="z%d" % n, tag=("c_g01" if n == 1 else "z%d" % n), align_bytes=64)
+            z[n] = keep.tile([P, CH, PACK], BF16, name="z%d" % n, tag=("c_g01" if n == 1 else "z%d" % n), align_bytes=256)
             nc.vector.tensor_tensor(
                 out=z[n][:].rearrange("p (c j) t -> p c t j", j=4),
                 in0=own[:].rearrange("p t (c j) -> p c t j", j=4),
@@ -241,7 +241,7 @@ def tile_list_pnet_bias_kernel(
         def second_layer(lo, hi, both_engines):
             for h in range(N // P):
                 y = psum.tile([P, hi - lo], F32, name="y%d_%d" % (lo, h), tag="bank%d" % {0: (7, 4), 256: (6, 5), 384: (0, 1)}[lo][h])
-                res = keep.tile([P, hi - lo], F32, name="res%d_%d" % (lo, h))
+                res = keep.tile([P, hi - lo], F32, name="res%d_%d" % (lo, h), align_bytes=256)
                 nc.tensor.matmul_mx(
                     out=y[:],
                     lhsT=wd_q[:, 2 * h * P : 2 * (h + 1) * P].bitcast(FP4X4),
@@ -261,7 +261,7 @@ def tile_list_pnet_bias_kernel(
             own_pass(n, 0)
         for n in range(2):
             own_pass(n, 1)
-        c_g01 = keep.tile([P, 256, PACK], BF16, name="c_g01", tag="c_g01", align_bytes=64)
+        c_g01 = keep.tile([P, 256, PACK], BF16, name="c_g01", tag="c_g01", align_bytes=256)
         nc.scalar.copy(out=c_g01[:].rearrange("p (c j) i -> p c i j", j=4), in_=c_raw[0, 1][:].rearrange("p i (c j) -> p c i j", j=4))
         nc.vector.quantize_mx(out=c_q[:, 0, 256:512].bitcast(FP8X4), scales=c_s[:, 0, 256:512], in_=c_g01[:].rearrange("p j i -> p (j i)"))
         own_pass(2, 0)

from contextlib import ExitStack

import concourse.mybir as mybir

K, R, N, T, J = 1024, 512, 256, 2048, 512
FLOPS = 2 * (3 * K * R * J + R * N * J)

F32 = mybir.dt.float32
BF16 = mybir.dt.bfloat16
I32 = mybir.dt.int32
U32 = mybir.dt.uint32
U16 = mybir.dt.uint16
U8 = mybir.dt.uint8
FP8X4 = mybir.dt.float8_e4m3fn_x4
FP4X4 = mybir.dt.float4_e2m1fn_x4
ALU = mybir.AluOpType
ACT = mybir.ActivationFunctionType

P = 128
PACK = 4
KP = P * PACK
PASSES = K // KP
CH = 128
SHIFT = 16


def tile_list_pnet_bias_kernel(
    tc, tab_words, tab_scales, c, w_words, w_scales, wc, wd_words, wd_scales, b, offs, out
):
    nc = tc.nc
    with ExitStack() as ctx:
        keep = ctx.enter_context(tc.tile_pool(name="keep", bufs=1))
        psum = ctx.enter_context(tc.psum_pool(name="psum", bufs=1))

        offsets = keep.tile([P, 2 * J // 16], U16, name="offsets")
        tab_s = keep.tile([P, T], U8, name="tab_s", align_bytes=256)
        tab_w = keep.tile([P, T], I32, name="tab_w", align_bytes=256)
        got_s = keep.tile([P, 2 * J], U8, name="got_s", align_bytes=256)
        got_s1 = keep.tile([P, 2 * J], U8, name="got_s1", align_bytes=256)
        w_raw = [keep.tile([P, R], I32, name="w_raw%d" % a, tag="w_raw%d" % a, align_bytes=256) for a in range(PASSES)]
        ws_raw = keep.tile([P, PASSES, R], U8, name="ws_raw", align_bytes=256)
        w_q = keep.tile([P, PASSES, R], I32, name="w_q", align_bytes=256)
        w_s = keep.tile([P, PASSES, R], U8, name="w_s", align_bytes=256)
        wd_q = keep.tile([P, 2 * N], U8, name="wd_q", align_bytes=256)
        wd_s = keep.tile([P, N], U8, name="wd_s", align_bytes=256)
        bias = keep.tile([P, N // P], F32, name="bias")

        nc.gpsimd.memset(ws_raw[:].rearrange("p a r -> p (a r)").bitcast(I32), 0)
        nc.gpsimd.memset(tab_s[:, 0 : T // 2].bitcast(I32), 0)
        nc.vector.memset(tab_s[:, T // 2 : T].bitcast(I32), 0)
        nc.vector.memset(wd_s[:].bitcast(I32), 0)
        nc.vector.memset(got_s1[:].bitcast(I32), 0)

        nc.sync.dma_start(offsets[:], offs)
        nc.sync.dma_start(out=ws_raw[0:16].bitcast(I32), in_=w_scales.bitcast(I32).rearrange("a q r -> q a r"))

        def load_w(a):
            nc.sync.dma_start(out=w_raw[a][:], in_=w_words[a].rearrange("p r i -> p (r i)").bitcast(I32))

        load_w(0)
        ts32 = tab_scales.bitcast(I32).rearrange("a (q r) t -> r q a t", r=4)
        for r in range(4):
            nc.sync.dma_start(out=tab_s[r:P:SHIFT, :].bitcast(I32), in_=ts32[r])
        nc.sync.dma_start(out=tab_w[:], in_=tab_words[0].rearrange("p t b -> p (t b)").bitcast(I32))

        def load_rows(src, a, lo, hi, name):
            raw = keep.tile([P, PACK, hi - lo], F32, name=name, tag=name, align_bytes=256)
            nc.sync.dma_start(out=raw[:], in_=src[a * KP : (a + 1) * KP, lo:hi].rearrange("(p i) w -> p i w", i=PACK))
            return raw

        nc.vector.tensor_copy(
            out=w_s[:].rearrange("p a (t m) -> p a t m", t=4),
            in_=ws_raw[:].rearrange("p a (m t) -> p a t m", t=4),
        )
        nc.vector.tensor_copy(out=got_s[:], in_=tab_s[:].indirect(offsets[:]))

        half = R // 2
        wc_whole = load_rows(wc, 0, 0, R, "wc_raw0")
        load_w(1)
        for q in range(1, 4):
            nc.sync.dma_start(out=w_s[32 * q : 32 * q + 4].bitcast(I32), in_=w_s[4 * q : 4 * q + 4].bitcast(I32))

        nc.sync.dma_start(out=got_s1[0 : P - SHIFT, :].bitcast(I32), in_=got_s[SHIFT:P, :].bitcast(I32))
        wc_raw = {(0, h): wc_whole[:, :, h * half : (h + 1) * half] for h in range(2)}
        for h in range(2):
            wc_raw[1, h] = load_rows(wc, 1, h * half, (h + 1) * half, "wc_raw1%d" % h)[:]
        c_raw = {}
        for h in range(2):
            for a in range(PASSES):
                c_raw[a, h] = load_rows(c, a, h * 256, (h + 1) * 256, "c_raw%d%d" % (a, h))
        nc.sync.dma_start(out=wd_q[:].bitcast(I32), in_=wd_words[0].bitcast(I32))
        for q in range(4):
            nc.sync.dma_start(out=wd_s[32 * q : 32 * q + 4, :].bitcast(I32), in_=wd_scales[0, 4 * q : 4 * q + 4, :].bitcast(I32))
        with nc.allow_non_contiguous_dma(reason="one bias value to a partition"):
            nc.sync.dma_start(out=bias[:], in_=b.rearrange("(h p) -> p h", p=P))

        cols = J // 16
        v_q = []

        got_w = []

        def look_up(g):
            gw = keep.tile([P, J], I32, name="got_w%d" % g, align_bytes=256)
            nc.vector.tensor_copy(out=gw[:].bitcast(U32), in_=tab_w[:].bitcast(U32).indirect(offsets[:, g * cols : (g + 1) * cols]))
            got_w.append(gw)

        def part(g):
            vq = keep.tile([P, PASSES, 2 * J], U8, name="v_q%d" % g, tag=("v_q0", "w_raw1")[g], align_bytes=256)
            nc.vector.tensor_copy(out=vq[:].bitcast(U16), in_=got_w[g][:].bitcast(U16).rearrange("p (j d) -> p d j", d=2))
            v_q.append(vq)

        look_up(0)
        part(0)
        look_up(1)
        for a in range(PASSES):
            nc.vector.tensor_copy(
                out=w_q[:, a, :].rearrange("p (t c i) -> p c t i", t=4, i=4),
                in_=w_raw[a][:].rearrange("p (c i t) -> p c t i", t=4, i=4),
            )
        part(1)

        wc_q = keep.tile([P, PASSES, R], U32, name="wc_q", align_bytes=256)
        wc_s = keep.tile([P, PASSES, R], U8, name="wc_s", align_bytes=256)
        wc_g = [keep.tile([P, 4, P, PACK], BF16, name="wc_g%d" % a, tag="wc_g%d" % a, align_bytes=256) for a in range(PASSES)]

        def wc_cast(move, a, lo, hi):
            at = lo % half
            move(
                out=wc_g[a][:, :, lo // 4 : hi // 4, :].rearrange("p t m i -> p m i t"),
                in_=wc_raw[a, lo // half][:, :, at : at + hi - lo].rearrange("p i (m t) -> p m i t", t=4),
            )

        def wc_quant(a):
            nc.vector.quantize_mx(out=wc_q[:, a, :].bitcast(FP8X4), scales=wc_s[:, a, :], in_=wc_g[a][:].rearrange("p t m i -> p (t m i)"))

        wc_cast(nc.scalar.copy, 0, 0, half)
        wc_cast(nc.scalar.copy, 0, half, R)
        wc_cast(nc.scalar.copy, 1, 0, 128)
        wc_cast(nc.vector.tensor_copy, 1, 128, half)
        wc_cast(nc.vector.tensor_copy, 1, half, R)
        wc_quant(0)
        wc_quant(1)

        c_q = keep.tile([P, PASSES, J], U32, name="c_q", align_bytes=256)
        c_s = keep.tile([P, PASSES, J], U8, name="c_s", align_bytes=256)
        c_g = keep.tile([P, PASSES, J, PACK], BF16, name="c_g", align_bytes=256)

        def c_piece(move, a, lo, hi):
            at = lo % 256
            move(
                out=c_g[:, a, lo:hi, :].rearrange("p (c j) i -> p c i j", j=4),
                in_=c_raw[a, lo // 256][:, :, at : at + hi - lo].rearrange("p i (c j) -> p c i j", j=4),
            )
            nc.vector.quantize_mx(out=c_q[:, a, lo:hi].bitcast(FP8X4), scales=c_s[:, a, lo:hi], in_=c_g[:, a, lo:hi, :].rearrange("p j i -> p (j i)"))

        pooled = keep.tile([P, 4, J], F32, name="pooled", tag="wc_raw11", align_bytes=256)
        planes = [got_s, got_s1]

        def neighbour(g, t, slot):
            bank = psum.tile([P, J], F32, name="a%d_%d" % (g, t), tag="bank%d" % slot)
            for a in range(PASSES):
                nc.tensor.matmul_mx(
                    out=bank[:],
                    lhsT=w_q[:, a, t * P : (t + 1) * P].bitcast(FP8X4),
                    lhsT_scale=w_s[:, a, t * P : (t + 1) * P],
                    rhs=v_q[g][:, a, :].bitcast(FP4X4),
                    rhs_scale=planes[a][:, g * J : (g + 1) * J],
                    start=(a == 0),
                    stop=(a == PASSES - 1),
                )
            return bank

        banks = [{0: neighbour(0, t, t)} for t in range(4)]
        for t in range(3):
            banks[t][1] = neighbour(1, t, 4 + t)
        early = keep.tile([P, 3, J], F32, name="first_early", tag="wc_raw10", align_bytes=256)
        first = [early[:, t, :] for t in range(3)]
        for t in range(3):
            nc.scalar.copy(out=first[t], in_=banks[t][0][:])

        def pool(t):
            nc.vector.tensor_tensor(out=pooled[:, t, :], in0=banks[t][1][:], in1=first[t], op=ALU.max)

        pool(0)
        pool(1)
        banks[3][1] = neighbour(1, 3, 5)
        pool(2)
        c_g00 = keep.tile([P, 256, PACK], BF16, name="c_g00", tag="wc_g1", align_bytes=256)
        nc.gpsimd.tensor_scalar(out=c_g00[:], in0=c_raw[0, 0][:].rearrange("p i j -> p j i"), scalar1=1.0, scalar2=0.0, op0=ALU.mult, op1=ALU.add)
        nc.vector.quantize_mx(out=c_q[:, 0, 0:256].bitcast(FP8X4), scales=c_s[:, 0, 0:256], in_=c_g00[:].rearrange("p j i -> p (j i)"))
        c_piece(nc.scalar.copy, 1, 0, 256)
        late = keep.tile([P, J], F32, name="first_late", tag="c_raw10", align_bytes=256)
        first.append(late[:])
        nc.scalar.copy(out=first[3], in_=banks[3][0][:])
        pool(3)

        z = {}
        hid = keep.tile([P, J * PACK], BF16, name="hid", tag="c_raw11", align_bytes=256)
        h_q = keep.tile([P, J], U32, name="h_q", align_bytes=256)
        h_s = keep.tile([P, J], U8, name="h_s", align_bytes=256)

        owns = {}

        def own_pass(n, a):
            tok = slice(n * CH, (n + 1) * CH)
            if a == 0:
                owns[n] = psum.tile([P, 4, CH], F32, name="own%d" % n, tag="bank%d" % n)
            for t in range(4):
                nc.tensor.matmul_mx(
                    out=owns[n][:, t, :],
                    lhsT=wc_q[:, a, t * P : (t + 1) * P].bitcast(FP8X4),
                    lhsT_scale=wc_s[:, a, t * P : (t + 1) * P],
                    rhs=c_q[:, a, tok].bitcast(FP8X4),
                    rhs_scale=c_s[:, a, tok],
                    start=(a == 0 and t == 0),
                    stop=(a == PASSES - 1 and t == 3),
                )

        def own_part(n):
            tok = slice(n * CH, (n + 1) * CH)
            own = owns[n]
            z[n] = keep.tile([P, CH, PACK], BF16, name="z%d" % n, tag=("c_g01" if n == 1 else "z%d" % n), align_bytes=256)
            nc.vector.tensor_tensor(
                out=z[n][:].rearrange("p (c j) t -> p c t j", j=4),
                in0=own[:].rearrange("p t (c j) -> p c t j", j=4),
                in1=pooled[:, :, tok].rearrange("p t (c j) -> p c t j", j=4),
                op=ALU.add,
            )

        def relu(n):
            src = z[n][:].rearrange("p j t -> p (j t)")
            dst = hid[:, PACK * CH * n : PACK * CH * (n + 1)]
            if n < 3:
                nc.scalar.activation(out=dst, in_=src, func=ACT.Relu)
            else:
                nc.vector.tensor_scalar_max(out=dst, in0=src, scalar1=0.0)

        def h_quant(lo, hi):
            nc.vector.quantize_mx(out=h_q[:, lo:hi].bitcast(FP8X4), scales=h_s[:, lo:hi], in_=hid[:, PACK * lo : PACK * hi])

        def second_layer(lo, hi, both_engines):
            for h in range(N // P):
                y = psum.tile([P, hi - lo], F32, name="y%d_%d" % (lo, h), tag="bank%d" % {0: (7, 4), 256: (6, 5), 384: (0, 1)}[lo][h])
                res = keep.tile([P, hi - lo], F32, name="res%d_%d" % (lo, h), align_bytes=256)
                nc.tensor.matmul_mx(
                    out=y[:],
                    lhsT=wd_q[:, 2 * h * P : 2 * (h + 1) * P].bitcast(FP4X4),
                    lhsT_scale=wd_s[:, h * P : (h + 1) * P],
                    rhs=h_q[:, lo:hi].bitcast(FP8X4),
                    rhs_scale=h_s[:, lo:hi],
                    start=True,
                    stop=True,
                )
                if both_engines and h == 1:
                    nc.vector.tensor_scalar_add(out=res[:], in0=y[:], scalar1=bias[:, h : h + 1])
                else:
                    nc.scalar.activation(out=res[:], in_=y[:], func=ACT.Identity, bias=bias[:, h : h + 1])
                nc.sync.dma_start(out=out[h * P : (h + 1) * P, lo:hi], in_=res[:])

        for n in range(2):
            own_pass(n, 0)
        for n in range(2):
            own_pass(n, 1)
        c_g01 = keep.tile([P, 256, PACK], BF16, name="c_g01", tag="c_g01", align_bytes=256)
        nc.scalar.copy(out=c_g01[:].rearrange("p (c j) i -> p c i j", j=4), in_=c_raw[0, 1][:].rearrange("p i (c j) -> p c i j", j=4))
        nc.vector.quantize_mx(out=c_q[:, 0, 256:512].bitcast(FP8X4), scales=c_s[:, 0, 256:512], in_=c_g01[:].rearrange("p j i -> p (j i)"))
        own_pass(2, 0)
        own_pass(3, 0)
        for n in (2, 3):
            c_piece(nc.scalar.copy if n == 2 else nc.vector.tensor_copy, 1, n * CH, (n + 1) * CH)
            own_pass(n, 1)
        for n in range(4):
            own_part(n)
        for n in range(4):
            relu(n)
        h_quant(0, 256)
        h_quant(256, 384)
        h_quant(384, 512)
        second_layer(0, 256, True)
        second_layer(256, 384, True)
        second_layer(384, 512, True)
